import numpy as np
import ml_dtypes


def mxq(x, axis, fmt="e4m3"):
    dtype, down = {"e4m3": (ml_dtypes.float8_e4m3fn, 7), "e5m2": (ml_dtypes.float8_e5m2, 14)}[fmt]
    v = np.moveaxis(np.asarray(x, np.float32).astype(ml_dtypes.bfloat16).astype(np.float64), axis, -1)
    blocks = v.reshape(v.shape[:-1] + (-1, 32))
    amax = np.abs(blocks).max(-1, keepdims=True)
    byte = np.maximum(np.where(amax > 0, np.frexp(amax)[1] - 1 + 127, 0) - down, 1)
    scale = np.exp2(byte - 127.0)
    codes = (blocks / scale).astype(np.float32).astype(dtype).astype(np.float64)
    return np.moveaxis((codes * scale).reshape(v.shape), -1, axis)


WIDE = False


def mx_kscale(k):
    if not WIDE:
        return np.ones(k)
    levels = np.array([10, -10, 5, -5, 0])
    if k % 512:
        return np.exp2(np.random.permutation(np.resize(levels, k // 32))).repeat(32)
    a = np.empty((k // 512, 16))
    for p in range(k // 512):
        a[p, :8] = np.random.permutation(np.resize(levels, 8))
        for g in range(8):
            far = levels[np.abs(levels - a[p, g]) >= 10]
            a[p, g + 8] = far[np.random.randint(len(far))]
    return np.exp2(a.ravel()).repeat(32)


def f64(x):
    return np.asarray(x).astype(np.float64)


def striped(idx):
    return np.tile(np.asarray(idx).reshape(-1, 16).T, (8, 1)).astype(np.uint16)


def unstriped(offs):
    return offs[:16].T.reshape(-1).astype(np.int64)


def striped8(idx):
    return np.asarray(idx).reshape(8, -1, 16).transpose(0, 2, 1).reshape(128, -1).astype(np.uint16)


def unstriped8(offs):
    return offs.reshape(8, 16, -1).transpose(0, 2, 1).reshape(8, -1).astype(np.int64)


def pick8(x, idx, run):
    r = np.arange(len(x))
    return x[r[:, None], idx[r % (8 * run) // run]]


E2M1 = np.array([0.0, 0.5, 1.0, 1.5, 2.0, 3.0, 4.0, 6.0, -0.0, -0.5, -1.0, -1.5, -2.0, -3.0, -4.0, -6.0])


def pack_weight(w, fmt):
    k, n = w.shape
    w = f64(np.asarray(w, np.float32).astype(ml_dtypes.bfloat16)).reshape(k // 32, 32, n)
    amax = np.abs(w).max(1)
    if fmt == "e4m3":
        byte = np.frexp(amax)[1] - 1 + 127 - 7
    else:
        mant, ex = np.frexp(amax / 6.0)
        byte = np.where(mant > 0.5, ex, ex - 1) + 127
    byte = np.clip(np.where(amax > 0, byte, 1), 1, 254)
    scaled = (w * np.exp2(127.0 - byte)[:, None, :]).reshape(k, n).astype(np.float32)
    by_word = np.ascontiguousarray(scaled.reshape(k // 512, 128, 4, n).transpose(0, 1, 3, 2))
    if fmt == "e4m3":
        words = by_word.astype(ml_dtypes.float8_e4m3fn).view(np.uint8)
    else:
        c = by_word.astype(ml_dtypes.float4_e2m1fn).view(np.uint8) & 0xF
        words = (c[..., 0::2] | (c[..., 1::2] << 4)).reshape(k // 512, 128, 2 * n)
    return np.ascontiguousarray(words), np.ascontiguousarray(byte.astype(np.uint8).reshape(k // 512, 16, n))


def unpack_weight(words, scales, fmt):
    g, _, n = scales.shape
    words = np.ascontiguousarray(words).reshape(g, 128, n, -1)
    if fmt == "e4m3":
        vals = words.view(ml_dtypes.float8_e4m3fn).astype(np.float64)
    else:
        nib = np.empty((g, 128, n, 4), np.uint8)
        nib[..., 0::2] = words & 0xF
        nib[..., 1::2] = words >> 4
        vals = E2M1[nib]
    vals = vals * np.repeat(np.exp2(scales.astype(np.float64) - 127.0), 8, axis=1)[..., None]
    return vals.transpose(0, 1, 3, 2).reshape(g * 512, n)


K, J, R, T, Z, M, O, N, U, E = 512, 512, 512, 1024, 512, 1024, 256, 256, 128, 512


def setup_inputs():
    n = np.random.standard_normal
    idx = np.stack([np.random.permutation(T)[:J] for _ in range(8)])
    idx2 = np.random.permutation(M)[:J]
    idx3 = np.random.permutation(J)[:O]
    idx4 = np.stack([np.random.permutation(J)[:O] for _ in range(8)])
    idx5 = np.random.permutation(E)[:O]
    idx6 = np.stack([np.random.permutation(E)[:U] for _ in range(8)])
    idx7 = np.stack([np.random.permutation(O)[:U] for _ in range(8)])
    fk = mx_kscale(K)
    fr = mx_kscale(R)
    fz = mx_kscale(Z)
    wp = pack_weight(n((K, R)) * 1 / np.sqrt(K) / fk[:, None] * fr, "e4m3")
    xop = pack_weight(n((Z, M)) / fz[:, None], "e4m3")
    w2p = pack_weight(n((Z, R)) * 1 / np.sqrt(Z) * fz[:, None] * fr, "e2m1")
    wbp = pack_weight(n((R, N)) * 1 / np.sqrt(R) / fr[:, None], "e2m1")
    wop = pack_weight(n((R, N)) * 1 / np.sqrt(R) / fr[:, None], "e4m3")
    return {
        "ta": (np.random.randint(-7, 8, (K, T)).astype(np.float64)).astype(np.float32),
        "ga": ((np.random.randint(8, 25, (K, 1)) / 64.0) * fk[:, None]).astype(np.float32),
        "w_words": wp[0],
        "w_scales": wp[1],
        "xo_words": xop[0],
        "xo_scales": xop[1],
        "w2_words": w2p[0],
        "w2_scales": w2p[1],
        "sa": (np.random.uniform(0.5, 1.6, (R, 1))).astype(np.float32),
        "sb": (np.random.uniform(0.5, 1.6, (R, 1))).astype(np.float32),
        "wb_words": wbp[0],
        "wb_scales": wbp[1],
        "wo_words": wop[0],
        "wo_scales": wop[1],
        "so": (np.random.uniform(0.5, 1.6, (N, 1))).astype(np.float32),
        "sp": (np.random.uniform(0.5, 1.6, (N, 1))).astype(np.float32),
        "offs": striped8(idx),
        "offs2": striped(idx2),
        "offs3": striped(idx3),
        "offs4": striped8(idx4),
        "offs5": striped(idx5),
        "offs6": striped8(idx6),
        "offs7": striped8(idx7),
    }


def reference(ta, ga, w_words, w_scales, xo_words, xo_scales, w2_words, w2_scales, sa, sb, wb_words, wb_scales, wo_words, wo_scales, so, sp, offs, offs2, offs3, offs4, offs5, offs6, offs7):
    idx = unstriped8(offs)
    idx2 = unstriped(offs2)
    idx3 = unstriped(offs3)
    idx4 = unstriped8(offs4)
    idx5 = unstriped(offs5)
    idx6 = unstriped8(offs6)
    idx7 = unstriped8(offs7)
    wu = unpack_weight(w_words, w_scales, "e4m3")
    xou = unpack_weight(xo_words, xo_scales, "e4m3")
    w2u = unpack_weight(w2_words, w2_scales, "e2m1")
    wbu = unpack_weight(wb_words, wb_scales, "e2m1")
    wou = unpack_weight(wo_words, wo_scales, "e4m3")
    xc = pick8(f64(ta), idx, 64) * f64(ga)
    xcq = mxq(xc, 0, "e4m3")
    xoidx2g = xou[:, idx2]
    a = wu.T @ xcq + w2u.T @ xoidx2g
    hid = np.abs(a[:, idx3] * f64(sa) - pick8(a, idx4, 64) * f64(sb))
    hidq = mxq(hid, 0, "e4m3")
    p = wbu.T @ hidq
    q = wou.T @ hidq
    m0 = np.zeros((N, E))
    m0[:, idx5] = p
    y = np.maximum(pick8(m0, idx6, 16) * f64(so), pick8(q, idx7, 16) * f64(sp))
    return y

@@ -1,0 +1,261 @@
+from contextlib import ExitStack
+
+import concourse.mybir as mybir
+
+K, J, R, T, Z, M, O, N, U, E = 512, 512, 512, 1024, 512, 1024, 256, 256, 128, 512
+FLOPS = 2 * (K * R * J + Z * R * J + 2 * R * N * O)
+
+F32 = mybir.dt.float32
+BF16 = mybir.dt.bfloat16
+I32 = mybir.dt.int32
+U32 = mybir.dt.uint32
+U16 = mybir.dt.uint16
+U8 = mybir.dt.uint8
+FP8X4 = mybir.dt.float8_e4m3fn_x4
+FP4X4 = mybir.dt.float4_e2m1fn_x4
+ACT = mybir.ActivationFunctionType
+ALU = mybir.AluOpType
+
+P = 128
+PACK = 4
+JH = J // 2
+OH = O // 2
+
+
+def tile_picked_codes_plain_bank_mixedpair_outcomes_outboard_kernel(
+    tc, ta, ga, w_words, w_scales, xo_words, xo_scales, w2_words, w2_scales, sa, sb,
+    wb_words, wb_scales, wo_words, wo_scales, so, sp,
+    offs, offs2, offs3, offs4, offs5, offs6, offs7, out,
+):
+    nc = tc.nc
+    with ExitStack() as ctx:
+        keep = ctx.enter_context(tc.tile_pool(name="keep", bufs=1))
+        psum = ctx.enter_context(tc.psum_pool(name="psum", bufs=1))
+
+        def sb_tile(name, shape, dtype):
+            return keep.tile(shape, dtype, name=name, align_bytes=64)
+
+        def load_list(name, src):
+            lst = keep.tile(list(src.shape), U16, name=name)
+            nc.sync.dma_start(lst[:], src)
+            return lst
+
+        def load_by_slot(name, src):
+            vec = sb_tile(name, [P, PACK], F32)
+            nc.sync.dma_start(vec[:], src.rearrange("(p t) o -> p (t o)", t=PACK))
+            return vec
+
+        def load_by_block(name, src):
+            vec = sb_tile(name, [P, 2], F32)
+            with nc.allow_non_contiguous_dma(reason="one value a partition"):
+                nc.sync.dma_start(vec[:], src.rearrange("(b p) o -> p (b o)", p=P))
+            return vec
+
+        def load_words(name, src2d, cols, dtype):
+            words = sb_tile(name, [P, cols], dtype)
+            nc.sync.dma_start(words[:].bitcast(I32), src2d.bitcast(I32))
+            return words
+
+        def stage_scales(name, src):
+            cols = src.shape[2]
+            staged = sb_tile(name, [4, 4, cols // 4], I32)
+            nc.sync.dma_start(staged[:], src[0].rearrange("(q r) n -> r q n", r=4).bitcast(I32))
+            return staged
+
+        def cleared_plane(name, cols):
+            plane = sb_tile(name, [P, cols], U8)
+            nc.vector.memset(plane[:].bitcast(I32), 0)
+            return plane
+
+        def spread_scales(plane, staged):
+            for q in range(4):
+                nc.vector.tensor_copy(plane[32 * q : 32 * q + 4, :].bitcast(I32), staged[:, q, :])
+
+        def deal(engine_copy, dealt, raw, run):
+            engine_copy(
+                dealt[:].rearrange("p t (c i) -> p c t i", i=run),
+                raw[:].rearrange("p (c i t) -> p c t i", i=run, t=PACK),
+            )
+
+        def interleave(grouped, planes):
+            nc.vector.tensor_copy(
+                grouped[:].rearrange("p (c i) t -> p c t i", i=4),
+                planes[:].rearrange("p t (c i) -> p c t i", i=4),
+            )
+
+        def quantise(name, grouped, cols):
+            codes = sb_tile(name + "_codes", [P, cols], U32)
+            scales = sb_tile(name + "_scales", [P, cols], U8)
+            nc.vector.quantize_mx(
+                out=codes[:].bitcast(FP8X4), scales=scales[:], in_=grouped[:].rearrange("p c t -> p (c t)")
+            )
+            return codes, scales
+
+        xo_plane = cleared_plane("xo_plane", M)
+        w2_plane = cleared_plane("w2_plane", R)
+        w_plane = cleared_plane("w_plane", R)
+        wb_plane = cleared_plane("wb_plane", N)
+        wo_plane = cleared_plane("wo_plane", N)
+        board = [sb_tile("board%d" % b, [P, E], F32) for b in range(2)]
+        for b in range(2):
+            nc.vector.memset(board[b][:], 0.0)
+
+        ta_rows = ta.rearrange("(p t) n -> t p n", t=PACK)
+        table = [sb_tile("table%d" % t, [P, T], F32) for t in range(PACK)]
+        l1 = load_list("l1", offs)
+        ga_t = load_by_slot("ga_t", ga)
+        nc.sync.dma_start(table[0][:], ta_rows[0])
+        xo_staged = stage_scales("xo_staged", xo_scales)
+        l2 = load_list("l2", offs2)
+        nc.sync.dma_start(table[1][:], ta_rows[1])
+        w2_staged = stage_scales("w2_staged", w2_scales)
+        w2_raw = load_words("w2_raw", w2_words[0], R, U16)
+        w_staged = stage_scales("w_staged", w_scales)
+        nc.sync.dma_start(table[2][:], ta_rows[2])
+        xo_raw = load_words("xo_raw", xo_words[0].rearrange("p n t -> p (n t)"), M, U32)
+        nc.sync.dma_start(table[3][:], ta_rows[3])
+        w_raw = load_words("w_raw", w_words[0].rearrange("p n t -> p (n t)"), R, U32)
+        sa_t = load_by_slot("sa_t", sa)
+        sb_t = load_by_slot("sb_t", sb)
+        l3 = load_list("l3", offs3)
+        l4 = load_list("l4", offs4)
+        wb_w = load_words("wb_w", wb_words[0], N, U16)
+        wo_w = load_words("wo_w", wo_words[0].rearrange("p n t -> p (n t)"), N, U32)
+        for plane, src in ((wb_plane, wb_scales), (wo_plane, wo_scales)):
+            rows = src[0].rearrange("(q r) n -> r q n", r=4).bitcast(I32)
+            for r in range(4):
+                nc.sync.dma_start(plane[r:P:32, :].bitcast(I32), rows[r])
+        l5 = load_list("l5", offs5)
+        l7 = load_list("l7", offs7)
+        sp_t = load_by_block("sp_t", sp)
+        l6 = load_list("l6", offs6)
+        so_t = load_by_block("so_t", so)
+
+        xc_planes = [sb_tile("xc_planes%d" % h, [P, PACK, JH], BF16) for h in range(2)]
+
+        def fetch_codes(t):
+            for h in range(2):
+                nc.scalar.activation(
+                    out=xc_planes[h][:, t, :],
+                    in_=table[t][:].indirect(l1[:, h * JH // 16 : (h + 1) * JH // 16]),
+                    func=ACT.Copy,
+                    scale=ga_t[:, t : t + 1],
+                )
+
+        fetch_codes(0)
+        spread_scales(xo_plane, xo_staged)
+        xo_s = sb_tile("xo_s", [P, J], U8)
+        nc.vector.tensor_copy(xo_s[:], xo_plane[:].indirect(l2[:]))
+        spread_scales(w2_plane, w2_staged)
+        w2_s = sb_tile("w2_s", [P, PACK, P], U8)
+        deal(nc.gpsimd.tensor_copy, w2_s, w2_plane, 16)
+        w2_w = sb_tile("w2_w", [P, PACK, P], U16)
+        deal(nc.scalar.copy, w2_w, w2_raw, 8)
+        spread_scales(w_plane, w_staged)
+        w_s = sb_tile("w_s", [P, PACK, P], U8)
+        deal(nc.gpsimd.tensor_copy, w_s, w_plane, 16)
+        xo_w = sb_tile("xo_w", [P, J], U32)
+        nc.vector.tensor_copy(xo_w[:], xo_raw[:].indirect(l2[:]))
+        for t in range(1, PACK):
+            fetch_codes(t)
+        w_w = sb_tile("w_w", [P, PACK, P], U32)
+        for pair in range(2):
+            nc.scalar.copy(
+                w_w[:, 2 * pair : 2 * pair + 2, :].rearrange("p t (c i) -> p c t i", i=4),
+                w_raw[:].rearrange("p (c i t) -> p c t i", i=4, t=PACK)[:, :, 2 * pair : 2 * pair + 2, :],
+            )
+
+        acc = [[psum.tile([P, JH], F32, name="acc", tag="bank%d" % (4 * h + t)) for t in range(PACK)] for h in range(2)]
+        for h in range(2):
+            cols = slice(h * JH, (h + 1) * JH)
+            for t in range(PACK):
+                nc.tensor.matmul_mx(
+                    out=acc[h][t][:], lhsT=w2_w[:, t, :].bitcast(FP4X4), lhsT_scale=w2_s[:, t, :],
+                    rhs=xo_w[:, cols].bitcast(FP8X4), rhs_scale=xo_s[:, cols], start=True, stop=False,
+                )
+        hidden = [sb_tile("hidden%d" % t, [P, J], F32) for t in range(PACK)]
+        for h in range(2):
+            cols = slice(h * JH, (h + 1) * JH)
+            grouped = sb_tile("xc_grouped%d" % h, [P, JH, PACK], BF16)
+            interleave(grouped, xc_planes[h])
+            xc_w, xc_s = quantise("xc%d" % h, grouped, JH)
+            for t in range(PACK):
+                nc.tensor.matmul_mx(
+                    out=acc[h][t][:], lhsT=w_w[:, t, :].bitcast(FP8X4), lhsT_scale=w_s[:, t, :],
+                    rhs=xc_w[:].bitcast(FP8X4), rhs_scale=xc_s[:], start=False, stop=True,
+                )
+                if h == 0:
+                    nc.scalar.copy(hidden[t][:, cols], acc[h][t][:])
+                else:
+                    nc.vector.tensor_copy(hidden[t][:, cols], acc[h][t][:])
+
+        second = [sb_tile("second%d" % b, [P, O], F32) for b in range(2)]
+
+        def places(u):
+            lcols = slice(u * OH // 16, (u + 1) * OH // 16)
+            g3 = sb_tile("g3_%d" % u, [P, PACK, OH], F32)
+            g4 = sb_tile("g4_%d" % u, [P, PACK, OH], F32)
+            diff = sb_tile("diff%d" % u, [P, PACK, OH], F32)
+            for t in range(PACK):
+                nc.scalar.activation(out=g3[:, t, :], in_=hidden[t][:].indirect(l3[:, lcols]), func=ACT.Copy, scale=sa_t[:, t : t + 1])
+                nc.scalar.activation(out=g4[:, t, :], in_=hidden[t][:].indirect(l4[:, lcols]), func=ACT.Copy, scale=sb_t[:, t : t + 1])
+            for ts in (slice(0, 2), slice(2, 3), slice(3, 4)):
+                nc.vector.tensor_tensor(diff[:, ts, :], g3[:, ts, :], g4[:, ts, :], ALU.subtract)
+            grouped = sb_tile("hid_grouped%d" % u, [P, OH, PACK], BF16)
+            by_place = diff[:].rearrange("p t o -> p o t")
+            nc.vector.scalar_tensor_tensor(grouped[:], by_place, -1.0, by_place, ALU.mult, ALU.max)
+            return quantise("hid%d" % u, grouped, OH)
+
+        def outcome(u, slot, words, dtype, plane, b, hid):
+            ncols = slice(b * P, (b + 1) * P)
+            res = psum.tile([P, OH], F32, name="res", tag="bank%d" % (4 * u + slot))
+            nc.tensor.matmul_mx(
+                out=res[:], lhsT=words[:, ncols].bitcast(dtype), lhsT_scale=plane[:, ncols],
+                rhs=hid[0][:].bitcast(FP8X4), rhs_scale=hid[1][:], start=True, stop=True,
+            )
+            return res
+
+        def outcomes(u, hid):
+            p1 = outcome(u, 0, wb_w, FP4X4, wb_plane, 1, hid)
+            q1 = outcome(u, 1, wo_w, FP8X4, wo_plane, 1, hid)
+            q0 = outcome(u, 2, wo_w, FP8X4, wo_plane, 0, hid)
+            p0 = outcome(u, 3, wb_w, FP4X4, wb_plane, 0, hid)
+            return [p0, p1], [q0, q1]
+
+        def held_tile(u, b):
+            return sb_tile("first%d_%d" % (u, b), [P, OH], F32)
+
+        early_list, late_list = l5[:, 0 : OH // 16], l5[:, OH // 16 : O // 16]
+        p_early, q_early = outcomes(0, places(0))
+        held_early = [held_tile(0, b) for b in range(2)]
+        p_late, q_late = outcomes(1, places(1))
+        for b in (0, 1):
+            nc.scalar.copy(held_early[b][:], p_early[b][:])
+            nc.scalar.activation(out=board[b][:].indirect(early_list), in_=held_early[b][:], func=ACT.Copy)
+        for b in (1, 0):
+            nc.vector.tensor_copy(second[b][:, 0:OH], q_early[b][:])
+        held_late = [held_tile(1, b) for b in range(2)]
+        nc.scalar.copy(held_late[1][:], p_late[1][:])
+        nc.scalar.activation(out=board[1][:].indirect(late_list), in_=held_late[1][:], func=ACT.Copy)
+        for b in (1, 0):
+            nc.vector.tensor_copy(second[b][:, OH:O], q_late[b][:])
+        nc.vector.tensor_copy(held_late[0][:], p_late[0][:])
+        nc.vector.tensor_copy(board[0][:].indirect(late_list), held_late[0][:])
+
+        left = [sb_tile("left%d" % b, [P, U], F32) for b in range(2)]
+        right = [sb_tile("right%d" % b, [P, U], F32) for b in range(2)]
+
+        def fetch_left(b):
+            nc.scalar.activation(out=left[b][:], in_=board[b][:].indirect(l6[:]), func=ACT.Copy, scale=so_t[:, b : b + 1])
+
+        def fetch_right(b):
+            nc.scalar.activation(out=right[b][:], in_=second[b][:].indirect(l7[:]), func=ACT.Copy, scale=sp_t[:, b : b + 1])
+
+        fetch_left(1)
+        fetch_right(1)
+        fetch_right(0)
+        fetch_left(0)
+        for b in (1, 0):
+            larger = sb_tile("larger%d" % b, [P, U], F32)
+            nc.vector.tensor_tensor(larger[:], left[b][:], right[b][:], ALU.max)
+            nc.sync.dma_start(out[b * P : (b + 1) * P, :], larger[:])

@@ -40,9 +40,9 @@ def tile_picked_codes_plain_bank_mixedpair_outcomes_outboard_kernel(
             nc.sync.dma_start(lst[:], src)
             return lst
 
-        def load_by_slot(name, src):
+        def load_by_slot(name, src, queue):
             vec = sb_tile(name, [P, PACK], F32)
-            nc.sync.dma_start(vec[:], src.rearrange("(p t) o -> p (t o)", t=PACK))
+            queue.dma_start(vec[:], src.rearrange("(p t) o -> p (t o)", t=PACK))
             return vec
 
         def load_by_block(name, src):
@@ -102,33 +102,31 @@ def tile_picked_codes_plain_bank_mixedpair_outcomes_outboard_kernel(
 
         ta_rows = ta.rearrange("(p t) n -> t p n", t=PACK)
         table = [sb_tile("table%d" % t, [P, T], F32) for t in range(PACK)]
+        nc.scalar.dma_start(table[0][:], ta_rows[0])
         l1 = load_list("l1", offs)
-        ga_t = load_by_slot("ga_t", ga)
-        nc.sync.dma_start(table[0][:], ta_rows[0])
+        ga_t = load_by_slot("ga_t", ga, nc.sync)
         xo_staged = stage_scales("xo_staged", xo_scales)
         l2 = load_list("l2", offs2)
         nc.sync.dma_start(table[1][:], ta_rows[1])
         w2_staged = stage_scales("w2_staged", w2_scales)
-        w2_raw = load_words("w2_raw", w2_words[0], R, U16)
-        w_staged = stage_scales("w_staged", w_scales)
         nc.sync.dma_start(table[2][:], ta_rows[2])
+        w_staged = stage_scales("w_staged", w_scales)
+        w2_raw = load_words("w2_raw", w2_words[0], R, U16)
         xo_raw = load_words("xo_raw", xo_words[0].rearrange("p n t -> p (n t)"), M, U32)
         nc.sync.dma_start(table[3][:], ta_rows[3])
         w_raw = load_words("w_raw", w_words[0].rearrange("p n t -> p (n t)"), R, U32)
-        sa_t = load_by_slot("sa_t", sa)
-        sb_t = load_by_slot("sb_t", sb)
         l3 = load_list("l3", offs3)
+        sa_t = load_by_slot("sa_t", sa, nc.sync)
         l4 = load_list("l4", offs4)
+        sb_t = load_by_slot("sb_t", sb, nc.sync)
+        wb_staged = stage_scales("wb_staged", wb_scales)
+        wo_staged = stage_scales("wo_staged", wo_scales)
         wb_w = load_words("wb_w", wb_words[0], N, U16)
         wo_w = load_words("wo_w", wo_words[0].rearrange("p n t -> p (n t)"), N, U32)
-        for plane, src in ((wb_plane, wb_scales), (wo_plane, wo_scales)):
-            rows = src[0].rearrange("(q r) n -> r q n", r=4).bitcast(I32)
-            for r in range(4):
-                nc.sync.dma_start(plane[r:P:32, :].bitcast(I32), rows[r])
         l5 = load_list("l5", offs5)
         l7 = load_list("l7", offs7)
-        sp_t = load_by_block("sp_t", sp)
         l6 = load_list("l6", offs6)
+        sp_t = load_by_block("sp_t", sp)
         so_t = load_by_block("so_t", so)
 
         xc_planes = [sb_tile("xc_planes%d" % h, [P, PACK, JH], BF16) for h in range(2)]
@@ -155,7 +153,10 @@ def tile_picked_codes_plain_bank_mixedpair_outcomes_outboard_kernel(
         w_s = sb_tile("w_s", [P, PACK, P], U8)
         deal(nc.gpsimd.tensor_copy, w_s, w_plane, 16)
         xo_w = sb_tile("xo_w", [P, J], U32)
-        nc.vector.tensor_copy(xo_w[:], xo_raw[:].indirect(l2[:]))
+        for h in range(2):
+            nc.vector.tensor_copy(
+                xo_w[:, h * JH : (h + 1) * JH], xo_raw[:].indirect(l2[:, h * JH // 16 : (h + 1) * JH // 16])
+            )
         for t in range(1, PACK):
             fetch_codes(t)
         w_w = sb_tile("w_w", [P, PACK, P], U32)
@@ -189,21 +190,24 @@ def tile_picked_codes_plain_bank_mixedpair_outcomes_outboard_kernel(
                 else:
                     nc.vector.tensor_copy(hidden[t][:, cols], acc[h][t][:])
 
+        spread_scales(wb_plane, wb_staged)
+        spread_scales(wo_plane, wo_staged)
         second = [sb_tile("second%d" % b, [P, O], F32) for b in range(2)]
 
         def places(u):
             lcols = slice(u * OH // 16, (u + 1) * OH // 16)
             g3 = sb_tile("g3_%d" % u, [P, PACK, OH], F32)
             g4 = sb_tile("g4_%d" % u, [P, PACK, OH], F32)
-            diff = sb_tile("diff%d" % u, [P, PACK, OH], F32)
+            diff = keep.tile([P, PACK, OH], F32, name="diff", tag="chain%d" % u, align_bytes=64)
             for t in range(PACK):
                 nc.scalar.activation(out=g3[:, t, :], in_=hidden[t][:].indirect(l3[:, lcols]), func=ACT.Copy, scale=sa_t[:, t : t + 1])
                 nc.scalar.activation(out=g4[:, t, :], in_=hidden[t][:].indirect(l4[:, lcols]), func=ACT.Copy, scale=sb_t[:, t : t + 1])
+            planes = sb_tile("hid_planes%d" % u, [P, PACK, OH], BF16)
             for ts in (slice(0, 2), slice(2, 3), slice(3, 4)):
                 nc.vector.tensor_tensor(diff[:, ts, :], g3[:, ts, :], g4[:, ts, :], ALU.subtract)
-            grouped = sb_tile("hid_grouped%d" % u, [P, OH, PACK], BF16)
-            by_place = diff[:].rearrange("p t o -> p o t")
-            nc.vector.scalar_tensor_tensor(grouped[:], by_place, -1.0, by_place, ALU.mult, ALU.max)
+                nc.vector.scalar_tensor_tensor(planes[:, ts, :], diff[:, ts, :], -1.0, diff[:, ts, :], ALU.mult, ALU.max)
+            grouped = keep.tile([P, OH, PACK], BF16, name="grouped", tag="chain%d" % (u + 1), align_bytes=64)
+            interleave(grouped, planes)
             return quantise("hid%d" % u, grouped, OH)
 
         def outcome(u, slot, words, dtype, plane, b, hid):

@@ -100,6 +100,10 @@ def tile_picked_codes_plain_bank_mixedpair_outcomes_outboard_kernel(
         for b in range(2):
             nc.vector.memset(board[b][:], 0.0)
 
+        warm_in = sb_tile("warm_in", [P, 8], F32)
+        warm_out = sb_tile("warm_out", [P, 8], F32)
+        nc.vector.memset(warm_in[:], 0.0)
+        nc.scalar.activation(out=warm_out[:], in_=warm_in[:], func=ACT.Copy)
         ta_rows = ta.rearrange("(p t) n -> t p n", t=PACK)
         table = [sb_tile("table%d" % t, [P, T], F32) for t in range(PACK)]
         nc.scalar.dma_start(table[0][:], ta_rows[0])

@@ -56,11 +56,24 @@ def tile_picked_codes_plain_bank_mixedpair_outcomes_outboard_kernel(
             nc.sync.dma_start(words[:].bitcast(I32), src2d.bitcast(I32))
             return words
 
-        def stage_scales(name, src):
+        def stage_scales(name, src, queue):
             cols = src.shape[2]
             staged = sb_tile(name, [4, 4, cols // 4], I32)
-            nc.sync.dma_start(staged[:], src[0].rearrange("(q r) n -> r q n", r=4).bitcast(I32))
+            queue.dma_start(staged[:], src[0].rearrange("(q r) n -> r q n", r=4).bitcast(I32))
             return staged
+
+        def stage_scales_by_halves(name, src):
+            cols = src.shape[2]
+            staged = sb_tile(name, [P, 2, cols // 4], I32)
+            rows = src[0].rearrange("(q r) n -> r q n", r=4).bitcast(I32)
+            for half in range(2):
+                nc.scalar.dma_start(staged[64 * half : 64 * half + 4, :, :], rows[:, 2 * half : 2 * half + 2, :])
+            return staged
+
+        def spread_scales_by_halves(plane, staged):
+            for q in range(4):
+                first = 64 * (q // 2)
+                nc.vector.tensor_copy(plane[32 * q : 32 * q + 4, :].bitcast(I32), staged[first : first + 4, q % 2, :])
 
         def cleared_plane(name, cols):
             plane = sb_tile(name, [P, cols], U8)
@@ -93,9 +106,9 @@ def tile_picked_codes_plain_bank_mixedpair_outcomes_outboard_kernel(
 
         xo_plane = cleared_plane("xo_plane", M)
         w2_plane = cleared_plane("w2_plane", R)
-        w_plane = cleared_plane("w_plane", R)
-        wb_plane = cleared_plane("wb_plane", N)
-        wo_plane = cleared_plane("wo_plane", N)
+        w_staged = sb_tile("w_staged", [P, 4, R // 4], I32)
+        nc.vector.memset(w_staged[64:96, :, :], 0)
+        out_plane = cleared_plane("out_plane", 2 * N)
         board = [sb_tile("board%d" % b, [P, E], F32) for b in range(2)]
         for b in range(2):
             nc.vector.memset(board[b][:], 0.0)
@@ -106,16 +119,16 @@ def tile_picked_codes_plain_bank_mixedpair_outcomes_outboard_kernel(
         nc.scalar.activation(out=warm_out[:], in_=warm_in[:], func=ACT.Copy)
         ta_rows = ta.rearrange("(p t) n -> t p n", t=PACK)
         table = [sb_tile("table%d" % t, [P, T], F32) for t in range(PACK)]
-        nc.scalar.dma_start(table[0][:], ta_rows[0])
+        xo_staged = stage_scales_by_halves("xo_staged", xo_scales)
+        w2_raw = load_words("w2_raw", w2_words[0], R, U16)
         l1 = load_list("l1", offs)
         ga_t = load_by_slot("ga_t", ga, nc.sync)
-        xo_staged = stage_scales("xo_staged", xo_scales)
-        l2 = load_list("l2", offs2)
+        nc.sync.dma_start(table[0][:], ta_rows[0])
+        w2_staged = stage_scales("w2_staged", w2_scales, nc.sync)
         nc.sync.dma_start(table[1][:], ta_rows[1])
-        w2_staged = stage_scales("w2_staged", w2_scales)
+        nc.sync.dma_start(w_staged[64:68, :, :], w_scales[0].rearrange("(q r) n -> r q n", r=4).bitcast(I32))
+        l2 = load_list("l2", offs2)
         nc.sync.dma_start(table[2][:], ta_rows[2])
-        w_staged = stage_scales("w_staged", w_scales)
-        w2_raw = load_words("w2_raw", w2_words[0], R, U16)
         xo_raw = load_words("xo_raw", xo_words[0].rearrange("p n t -> p (n t)"), M, U32)
         nc.sync.dma_start(table[3][:], ta_rows[3])
         w_raw = load_words("w_raw", w_words[0].rearrange("p n t -> p (n t)"), R, U32)
@@ -123,11 +136,12 @@ def tile_picked_codes_plain_bank_mixedpair_outcomes_outboard_kernel(
         sa_t = load_by_slot("sa_t", sa, nc.sync)
         l4 = load_list("l4", offs4)
         sb_t = load_by_slot("sb_t", sb, nc.sync)
-        wb_staged = stage_scales("wb_staged", wb_scales)
-        wo_staged = stage_scales("wo_staged", wo_scales)
+        out_staged = sb_tile("out_staged", [4, 4, 2, N // 4], I32)
+        for which, src in enumerate((wb_scales, wo_scales)):
+            nc.sync.dma_start(out_staged[:, :, which, :], src[0].rearrange("(q r) n -> r q n", r=4).bitcast(I32))
+        l5 = load_list("l5", offs5)
         wb_w = load_words("wb_w", wb_words[0], N, U16)
         wo_w = load_words("wo_w", wo_words[0].rearrange("p n t -> p (n t)"), N, U32)
-        l5 = load_list("l5", offs5)
         l7 = load_list("l7", offs7)
         l6 = load_list("l6", offs6)
         sp_t = load_by_block("sp_t", sp)
@@ -144,24 +158,27 @@ def tile_picked_codes_plain_bank_mixedpair_outcomes_outboard_kernel(
                     scale=ga_t[:, t : t + 1],
                 )
 
+        w2_w = sb_tile("w2_w", [P, PACK, P], U16)
+        deal(nc.scalar.copy, w2_w, w2_raw, 8)
         fetch_codes(0)
-        spread_scales(xo_plane, xo_staged)
+        fetch_codes(1)
+        spread_scales_by_halves(xo_plane, xo_staged)
         xo_s = sb_tile("xo_s", [P, J], U8)
-        nc.vector.tensor_copy(xo_s[:], xo_plane[:].indirect(l2[:]))
         spread_scales(w2_plane, w2_staged)
         w2_s = sb_tile("w2_s", [P, PACK, P], U8)
         deal(nc.gpsimd.tensor_copy, w2_s, w2_plane, 16)
-        w2_w = sb_tile("w2_w", [P, PACK, P], U16)
-        deal(nc.scalar.copy, w2_w, w2_raw, 8)
-        spread_scales(w_plane, w_staged)
+        w_plane = sb_tile("w_plane", [P, R], U8)
+        for q in range(4):
+            nc.vector.tensor_copy(w_plane[32 * q : 32 * q + 32, :].bitcast(I32), w_staged[64:96, q, :])
         w_s = sb_tile("w_s", [P, PACK, P], U8)
         deal(nc.gpsimd.tensor_copy, w_s, w_plane, 16)
+        nc.vector.tensor_copy(xo_s[:], xo_plane[:].indirect(l2[:]))
         xo_w = sb_tile("xo_w", [P, J], U32)
         for h in range(2):
             nc.vector.tensor_copy(
                 xo_w[:, h * JH : (h + 1) * JH], xo_raw[:].indirect(l2[:, h * JH // 16 : (h + 1) * JH // 16])
             )
-        for t in range(1, PACK):
+        for t in range(2, PACK):
             fetch_codes(t)
         w_w = sb_tile("w_w", [P, PACK, P], U32)
         for pair in range(2):
@@ -194,22 +211,27 @@ def tile_picked_codes_plain_bank_mixedpair_outcomes_outboard_kernel(
                 else:
                     nc.vector.tensor_copy(hidden[t][:, cols], acc[h][t][:])
 
-        spread_scales(wb_plane, wb_staged)
-        spread_scales(wo_plane, wo_staged)
+        for q in range(4):
+            nc.vector.tensor_copy(
+                out_plane[32 * q : 32 * q + 4, :].bitcast(I32), out_staged[:, q, :, :].rearrange("r w n -> r (w n)")
+            )
+        wb_plane, wo_plane = out_plane[:, 0:N], out_plane[:, N : 2 * N]
         second = [sb_tile("second%d" % b, [P, O], F32) for b in range(2)]
 
         def places(u):
             lcols = slice(u * OH // 16, (u + 1) * OH // 16)
-            g3 = sb_tile("g3_%d" % u, [P, PACK, OH], F32)
-            g4 = sb_tile("g4_%d" % u, [P, PACK, OH], F32)
             diff = keep.tile([P, PACK, OH], F32, name="diff", tag="chain%d" % u, align_bytes=64)
-            for t in range(PACK):
-                nc.scalar.activation(out=g3[:, t, :], in_=hidden[t][:].indirect(l3[:, lcols]), func=ACT.Copy, scale=sa_t[:, t : t + 1])
-                nc.scalar.activation(out=g4[:, t, :], in_=hidden[t][:].indirect(l4[:, lcols]), func=ACT.Copy, scale=sb_t[:, t : t + 1])
             planes = sb_tile("hid_planes%d" % u, [P, PACK, OH], BF16)
-            for ts in (slice(0, 2), slice(2, 3), slice(3, 4)):
-                nc.vector.tensor_tensor(diff[:, ts, :], g3[:, ts, :], g4[:, ts, :], ALU.subtract)
-                nc.vector.scalar_tensor_tensor(planes[:, ts, :], diff[:, ts, :], -1.0, diff[:, ts, :], ALU.mult, ALU.max)
+            for piece, ts in enumerate((range(0, 2), range(2, 3), range(3, 4))):
+                ring = (piece + u) % 3
+                g3 = keep.tile([P, len(ts), OH], F32, name="g3", tag="g3_%d" % ring, align_bytes=64)
+                g4 = keep.tile([P, len(ts), OH], F32, name="g4", tag="g4_%d" % ring, align_bytes=64)
+                for i, t in enumerate(ts):
+                    nc.scalar.activation(out=g3[:, i, :], in_=hidden[t][:].indirect(l3[:, lcols]), func=ACT.Copy, scale=sa_t[:, t : t + 1])
+                    nc.scalar.activation(out=g4[:, i, :], in_=hidden[t][:].indirect(l4[:, lcols]), func=ACT.Copy, scale=sb_t[:, t : t + 1])
+                rows = slice(ts.start, ts.stop)
+                nc.vector.tensor_tensor(diff[:, rows, :], g3[:], g4[:], ALU.subtract)
+                nc.vector.scalar_tensor_tensor(planes[:, rows, :], diff[:, rows, :], -1.0, diff[:, rows, :], ALU.mult, ALU.max)
             grouped = keep.tile([P, OH, PACK], BF16, name="grouped", tag="chain%d" % (u + 1), align_bytes=64)
             interleave(grouped, planes)
             return quantise("hid%d" % u, grouped, OH)
@@ -225,9 +247,9 @@ def tile_picked_codes_plain_bank_mixedpair_outcomes_outboard_kernel(
 
         def outcomes(u, hid):
             p1 = outcome(u, 0, wb_w, FP4X4, wb_plane, 1, hid)
-            q1 = outcome(u, 1, wo_w, FP8X4, wo_plane, 1, hid)
-            q0 = outcome(u, 2, wo_w, FP8X4, wo_plane, 0, hid)
-            p0 = outcome(u, 3, wb_w, FP4X4, wb_plane, 0, hid)
+            p0 = outcome(u, 1, wb_w, FP4X4, wb_plane, 0, hid)
+            q1 = outcome(u, 2, wo_w, FP8X4, wo_plane, 1, hid)
+            q0 = outcome(u, 3, wo_w, FP8X4, wo_plane, 0, hid)
             return [p0, p1], [q0, q1]
 
         def held_tile(u, b):
@@ -236,19 +258,20 @@ def tile_picked_codes_plain_bank_mixedpair_outcomes_outboard_kernel(
         early_list, late_list = l5[:, 0 : OH // 16], l5[:, OH // 16 : O // 16]
         p_early, q_early = outcomes(0, places(0))
         held_early = [held_tile(0, b) for b in range(2)]
+        for b in (1, 0):
+            nc.vector.tensor_copy(held_early[b][:], p_early[b][:])
         p_late, q_late = outcomes(1, places(1))
-        for b in (0, 1):
-            nc.scalar.copy(held_early[b][:], p_early[b][:])
+        for b in (1, 0):
             nc.scalar.activation(out=board[b][:].indirect(early_list), in_=held_early[b][:], func=ACT.Copy)
         for b in (1, 0):
             nc.vector.tensor_copy(second[b][:, 0:OH], q_early[b][:])
         held_late = [held_tile(1, b) for b in range(2)]
-        nc.scalar.copy(held_late[1][:], p_late[1][:])
-        nc.scalar.activation(out=board[1][:].indirect(late_list), in_=held_late[1][:], func=ACT.Copy)
+        nc.vector.tensor_copy(held_late[1][:], p_late[1][:])
+        nc.scalar.copy(held_late[0][:], p_late[0][:])
         for b in (1, 0):
-            nc.vector.tensor_copy(second[b][:, OH:O], q_late[b][:])
-        nc.vector.tensor_copy(held_late[0][:], p_late[0][:])
-        nc.vector.tensor_copy(board[0][:].indirect(late_list), held_late[0][:])
+            nc.vector.tensor_copy(board[b][:].indirect(late_list), held_late[b][:])
+        for b in (1, 0):
+            nc.scalar.copy(second[b][:, OH:O], q_late[b][:])
 
         left = [sb_tile("left%d" % b, [P, U], F32) for b in range(2)]
         right = [sb_tile("right%d" % b, [P, U], F32) for b in range(2)]
@@ -259,9 +282,9 @@ def tile_picked_codes_plain_bank_mixedpair_outcomes_outboard_kernel(
         def fetch_right(b):
             nc.scalar.activation(out=right[b][:], in_=second[b][:].indirect(l7[:]), func=ACT.Copy, scale=sp_t[:, b : b + 1])
 
-        fetch_left(1)
         fetch_right(1)
         fetch_right(0)
+        fetch_left(1)
         fetch_left(0)
         for b in (1, 0):
             larger = sb_tile("larger%d" % b, [P, U], F32)

from contextlib import ExitStack

import concourse.mybir as mybir

K, J, R, T, Z, M, O, N, U, E = 512, 512, 512, 1024, 512, 1024, 256, 256, 128, 512
FLOPS = 2 * (K * R * J + Z * R * J + 2 * R * N * O)

F32 = mybir.dt.float32
BF16 = mybir.dt.bfloat16
I32 = mybir.dt.int32
U32 = mybir.dt.uint32
U16 = mybir.dt.uint16
U8 = mybir.dt.uint8
FP8X4 = mybir.dt.float8_e4m3fn_x4
FP4X4 = mybir.dt.float4_e2m1fn_x4
ACT = mybir.ActivationFunctionType
ALU = mybir.AluOpType

P = 128
PACK = 4
JH = J // 2
OH = O // 2


def tile_picked_codes_plain_bank_mixedpair_outcomes_outboard_kernel(
    tc, ta, ga, w_words, w_scales, xo_words, xo_scales, w2_words, w2_scales, sa, sb,
    wb_words, wb_scales, wo_words, wo_scales, so, sp,
    offs, offs2, offs3, offs4, offs5, offs6, offs7, out,
):
    nc = tc.nc
    with ExitStack() as ctx:
        keep = ctx.enter_context(tc.tile_pool(name="keep", bufs=1))
        psum = ctx.enter_context(tc.psum_pool(name="psum", bufs=1))

        def sb_tile(name, shape, dtype):
            return keep.tile(shape, dtype, name=name, align_bytes=64)

        def load_list(name, src):
            lst = keep.tile(list(src.shape), U16, name=name)
            nc.sync.dma_start(lst[:], src)
            return lst

        def load_by_slot(name, src, queue):
            vec = sb_tile(name, [P, PACK], F32)
            queue.dma_start(vec[:], src.rearrange("(p t) o -> p (t o)", t=PACK))
            return vec

        def load_by_block(name, src):
            vec = sb_tile(name, [P, 2], F32)
            with nc.allow_non_contiguous_dma(reason="one value a partition"):
                nc.sync.dma_start(vec[:], src.rearrange("(b p) o -> p (b o)", p=P))
            return vec

        def load_words(name, src2d, cols, dtype):
            words = sb_tile(name, [P, cols], dtype)
            nc.sync.dma_start(words[:].bitcast(I32), src2d.bitcast(I32))
            return words

        def stage_scales(name, src, queue):
            cols = src.shape[2]
            staged = sb_tile(name, [4, 4, cols // 4], I32)
            queue.dma_start(staged[:], src[0].rearrange("(q r) n -> r q n", r=4).bitcast(I32))
            return staged

        def stage_scales_by_halves(name, src):
            cols = src.shape[2]
            staged = sb_tile(name, [P, 2, cols // 4], I32)
            rows = src[0].rearrange("(q r) n -> r q n", r=4).bitcast(I32)
            for half in range(2):
                nc.scalar.dma_start(staged[64 * half : 64 * half + 4, :, :], rows[:, 2 * half : 2 * half + 2, :])
            return staged

        def spread_scales_by_halves(plane, staged):
            for q in range(4):
                first = 64 * (q // 2)
                nc.vector.tensor_copy(plane[32 * q : 32 * q + 4, :].bitcast(I32), staged[first : first + 4, q % 2, :])

        def cleared_plane(name, cols):
            plane = sb_tile(name, [P, cols], U8)
            nc.vector.memset(plane[:].bitcast(I32), 0)
            return plane

        def spread_scales(plane, staged):
            for q in range(4):
                nc.vector.tensor_copy(plane[32 * q : 32 * q + 4, :].bitcast(I32), staged[:, q, :])

        def deal(engine_copy, dealt, raw, run):
            engine_copy(
                dealt[:].rearrange("p t (c i) -> p c t i", i=run),
                raw[:].rearrange("p (c i t) -> p c t i", i=run, t=PACK),
            )

        def interleave(grouped, planes):
            nc.vector.tensor_copy(
                grouped[:].rearrange("p (c i) t -> p c t i", i=4),
                planes[:].rearrange("p t (c i) -> p c t i", i=4),
            )

        def quantise(name, grouped, cols):
            codes = sb_tile(name + "_codes", [P, cols], U32)
            scales = sb_tile(name + "_scales", [P, cols], U8)
            nc.vector.quantize_mx(
                out=codes[:].bitcast(FP8X4), scales=scales[:], in_=grouped[:].rearrange("p c t -> p (c t)")
            )
            return codes, scales

        xo_plane = cleared_plane("xo_plane", M)
        w2_plane = cleared_plane("w2_plane", R)
        w_staged = sb_tile("w_staged", [P, 4, R // 4], I32)
        nc.vector.memset(w_staged[64:96, :, :], 0)
        out_plane = cleared_plane("out_plane", 2 * N)
        board = [sb_tile("board%d" % b, [P, E], F32) for b in range(2)]
        for b in range(2):
            nc.vector.memset(board[b][:], 0.0)

        warm_in = sb_tile("warm_in", [P, 8], F32)
        warm_out = sb_tile("warm_out", [P, 8], F32)
        nc.vector.memset(warm_in[:], 0.0)
        nc.scalar.activation(out=warm_out[:], in_=warm_in[:], func=ACT.Copy)
        ta_rows = ta.rearrange("(p t) n -> t p n", t=PACK)
        table = [sb_tile("table%d" % t, [P, T], F32) for t in range(PACK)]
        xo_staged = stage_scales_by_halves("xo_staged", xo_scales)
        w2_raw = load_words("w2_raw", w2_words[0], R, U16)
        l1 = load_list("l1", offs)
        ga_t = load_by_slot("ga_t", ga, nc.sync)
        nc.sync.dma_start(table[0][:], ta_rows[0])
        w2_staged = stage_scales("w2_staged", w2_scales, nc.sync)
        nc.sync.dma_start(table[1][:], ta_rows[1])
        nc.sync.dma_start(w_staged[64:68, :, :], w_scales[0].rearrange("(q r) n -> r q n", r=4).bitcast(I32))
        l2 = load_list("l2", offs2)
        nc.sync.dma_start(table[2][:], ta_rows[2])
        xo_raw = load_words("xo_raw", xo_words[0].rearrange("p n t -> p (n t)"), M, U32)
        nc.sync.dma_start(table[3][:], ta_rows[3])
        w_raw = load_words("w_raw", w_words[0].rearrange("p n t -> p (n t)"), R, U32)
        l3 = load_list("l3", offs3)
        sa_t = load_by_slot("sa_t", sa, nc.sync)
        l4 = load_list("l4", offs4)
        sb_t = load_by_slot("sb_t", sb, nc.sync)
        out_staged = sb_tile("out_staged", [4, 4, 2, N // 4], I32)
        for which, src in enumerate((wb_scales, wo_scales)):
            nc.sync.dma_start(out_staged[:, :, which, :], src[0].rearrange("(q r) n -> r q n", r=4).bitcast(I32))
        l5 = load_list("l5", offs5)
        wb_w = load_words("wb_w", wb_words[0], N, U16)
        wo_w = load_words("wo_w", wo_words[0].rearrange("p n t -> p (n t)"), N, U32)
        l7 = load_list("l7", offs7)
        l6 = load_list("l6", offs6)
        sp_t = load_by_block("sp_t", sp)
        so_t = load_by_block("so_t", so)

        xc_planes = [sb_tile("xc_planes%d" % h, [P, PACK, JH], BF16) for h in range(2)]

        def fetch_codes(t):
            for h in range(2):
                nc.scalar.activation(
                    out=xc_planes[h][:, t, :],
                    in_=table[t][:].indirect(l1[:, h * JH // 16 : (h + 1) * JH // 16]),
                    func=ACT.Copy,
                    scale=ga_t[:, t : t + 1],
                )

        w2_w = sb_tile("w2_w", [P, PACK, P], U16)
        deal(nc.scalar.copy, w2_w, w2_raw, 8)
        fetch_codes(0)
        fetch_codes(1)
        spread_scales_by_halves(xo_plane, xo_staged)
        xo_s = sb_tile("xo_s", [P, J], U8)
        spread_scales(w2_plane, w2_staged)
        w2_s = sb_tile("w2_s", [P, PACK, P], U8)
        deal(nc.gpsimd.tensor_copy, w2_s, w2_plane, 16)
        w_plane = sb_tile("w_plane", [P, R], U8)
        for q in range(4):
            nc.vector.tensor_copy(w_plane[32 * q : 32 * q + 32, :].bitcast(I32), w_staged[64:96, q, :])
        w_s = sb_tile("w_s", [P, PACK, P], U8)
        deal(nc.gpsimd.tensor_copy, w_s, w_plane, 16)
        nc.vector.tensor_copy(xo_s[:], xo_plane[:].indirect(l2[:]))
        xo_w = sb_tile("xo_w", [P, J], U32)
        for h in range(2):
            nc.vector.tensor_copy(
                xo_w[:, h * JH : (h + 1) * JH], xo_raw[:].indirect(l2[:, h * JH // 16 : (h + 1) * JH // 16])
            )
        for t in range(2, PACK):
            fetch_codes(t)
        w_w = sb_tile("w_w", [P, PACK, P], U32)
        for pair in range(2):
            nc.scalar.copy(
                w_w[:, 2 * pair : 2 * pair + 2, :].rearrange("p t (c i) -> p c t i", i=4),
                w_raw[:].rearrange("p (c i t) -> p c t i", i=4, t=PACK)[:, :, 2 * pair : 2 * pair + 2, :],
            )

        acc = [[psum.tile([P, JH], F32, name="acc", tag="bank%d" % (4 * h + t)) for t in range(PACK)] for h in range(2)]
        for h in range(2):
            cols = slice(h * JH, (h + 1) * JH)
            for t in range(PACK):
                nc.tensor.matmul_mx(
                    out=acc[h][t][:], lhsT=w2_w[:, t, :].bitcast(FP4X4), lhsT_scale=w2_s[:, t, :],
                    rhs=xo_w[:, cols].bitcast(FP8X4), rhs_scale=xo_s[:, cols], start=True, stop=False,
                )
        hidden = [sb_tile("hidden%d" % t, [P, J], F32) for t in range(PACK)]
        for h in range(2):
            cols = slice(h * JH, (h + 1) * JH)
            grouped = sb_tile("xc_grouped%d" % h, [P, JH, PACK], BF16)
            interleave(grouped, xc_planes[h])
            xc_w, xc_s = quantise("xc%d" % h, grouped, JH)
            for t in range(PACK):
                nc.tensor.matmul_mx(
                    out=acc[h][t][:], lhsT=w_w[:, t, :].bitcast(FP8X4), lhsT_scale=w_s[:, t, :],
                    rhs=xc_w[:].bitcast(FP8X4), rhs_scale=xc_s[:], start=False, stop=True,
                )
                if h == 0:
                    nc.scalar.copy(hidden[t][:, cols], acc[h][t][:])
                else:
                    nc.vector.tensor_copy(hidden[t][:, cols], acc[h][t][:])

        for q in range(4):
            nc.vector.tensor_copy(
                out_plane[32 * q : 32 * q + 4, :].bitcast(I32), out_staged[:, q, :, :].rearrange("r w n -> r (w n)")
            )
        wb_plane, wo_plane = out_plane[:, 0:N], out_plane[:, N : 2 * N]
        second = [sb_tile("second%d" % b, [P, O], F32) for b in range(2)]

        def places(u):
            lcols = slice(u * OH // 16, (u + 1) * OH // 16)
            diff = keep.tile([P, PACK, OH], F32, name="diff", tag="chain%d" % u, align_bytes=64)
            planes = sb_tile("hid_planes%d" % u, [P, PACK, OH], BF16)
            for piece, ts in enumerate((range(0, 2), range(2, 3), range(3, 4))):
                ring = (piece + u) % 3
                g3 = keep.tile([P, len(ts), OH], F32, name="g3", tag="g3_%d" % ring, align_bytes=64)
                g4 = keep.tile([P, len(ts), OH], F32, name="g4", tag="g4_%d" % ring, align_bytes=64)
                for i, t in enumerate(ts):
                    nc.scalar.activation(out=g3[:, i, :], in_=hidden[t][:].indirect(l3[:, lcols]), func=ACT.Copy, scale=sa_t[:, t : t + 1])
                    nc.scalar.activation(out=g4[:, i, :], in_=hidden[t][:].indirect(l4[:, lcols]), func=ACT.Copy, scale=sb_t[:, t : t + 1])
                rows = slice(ts.start, ts.stop)
                nc.vector.tensor_tensor(diff[:, rows, :], g3[:], g4[:], ALU.subtract)
                nc.vector.scalar_tensor_tensor(planes[:, rows, :], diff[:, rows, :], -1.0, diff[:, rows, :], ALU.mult, ALU.max)
            grouped = keep.tile([P, OH, PACK], BF16, name="grouped", tag="chain%d" % (u + 1), align_bytes=64)
            interleave(grouped, planes)
            return quantise("hid%d" % u, grouped, OH)

        def outcome(u, slot, words, dtype, plane, b, hid):
            ncols = slice(b * P, (b + 1) * P)
            res = psum.tile([P, OH], F32, name="res", tag="bank%d" % (4 * u + slot))
            nc.tensor.matmul_mx(
                out=res[:], lhsT=words[:, ncols].bitcast(dtype), lhsT_scale=plane[:, ncols],
                rhs=hid[0][:].bitcast(FP8X4), rhs_scale=hid[1][:], start=True, stop=True,
            )
            return res

        def outcomes(u, hid):
            p1 = outcome(u, 0, wb_w, FP4X4, wb_plane, 1, hid)
            p0 = outcome(u, 1, wb_w, FP4X4, wb_plane, 0, hid)
            q1 = outcome(u, 2, wo_w, FP8X4, wo_plane, 1, hid)
            q0 = outcome(u, 3, wo_w, FP8X4, wo_plane, 0, hid)
            return [p0, p1], [q0, q1]

        def held_tile(u, b):
            return sb_tile("first%d_%d" % (u, b), [P, OH], F32)

        early_list, late_list = l5[:, 0 : OH // 16], l5[:, OH // 16 : O // 16]
        p_early, q_early = outcomes(0, places(0))
        held_early = [held_tile(0, b) for b in range(2)]
        for b in (1, 0):
            nc.vector.tensor_copy(held_early[b][:], p_early[b][:])
        p_late, q_late = outcomes(1, places(1))
        for b in (1, 0):
            nc.scalar.activation(out=board[b][:].indirect(early_list), in_=held_early[b][:], func=ACT.Copy)
        for b in (1, 0):
            nc.vector.tensor_copy(second[b][:, 0:OH], q_early[b][:])
        held_late = [held_tile(1, b) for b in range(2)]
        nc.vector.tensor_copy(held_late[1][:], p_late[1][:])
        nc.scalar.copy(held_late[0][:], p_late[0][:])
        for b in (1, 0):
            nc.vector.tensor_copy(board[b][:].indirect(late_list), held_late[b][:])
        for b in (1, 0):
            nc.scalar.copy(second[b][:, OH:O], q_late[b][:])

        left = [sb_tile("left%d" % b, [P, U], F32) for b in range(2)]
        right = [sb_tile("right%d" % b, [P, U], F32) for b in range(2)]

        def fetch_left(b):
            nc.scalar.activation(out=left[b][:], in_=board[b][:].indirect(l6[:]), func=ACT.Copy, scale=so_t[:, b : b + 1])

        def fetch_right(b):
            nc.scalar.activation(out=right[b][:], in_=second[b][:].indirect(l7[:]), func=ACT.Copy, scale=sp_t[:, b : b + 1])

        fetch_right(1)
        fetch_right(0)
        fetch_left(1)
        fetch_left(0)
        for b in (1, 0):
            larger = sb_tile("larger%d" % b, [P, U], F32)
            nc.vector.tensor_tensor(larger[:], left[b][:], right[b][:], ALU.max)
            nc.sync.dma_start(out[b * P : (b + 1) * P, :], larger[:])
